import numpy as np, ml_dtypes
CORES = [72,73,74,75,76,77,78,79,64,65,66,67]
N = 12
def setup_inputs(rng):
    return {"x": rng.standard_normal((N, 128, 8), dtype=np.float32).astype(ml_dtypes.bfloat16)}
def reference(x):
    g = np.concatenate(list(x), axis=1)
    return {"y": np.broadcast_to(g, (N,) + g.shape)}

@@ -1,0 +1,59 @@
+from concourse.bass import DstId, RemoteDMATransfer
+
+SCRATCH = {
+    "g": ("sbuf", [128, 96], "bfloat16"),
+}
+SEMAPHORES = ["ld", "st", "on", "xc", "fan", "sent"]
+
+B = 8
+CROSS = {74: (0, 64), 75: (2, 65), 78: (4, 66), 79: (6, 67), 67: (10, 72), 70: (8, 76)}
+HELPER_FEED = {64: 70, 65: 70}
+
+
+def rank_program(g, core, T, topo):
+    rank = T.rank_of(core)
+    if rank is None and core != 70:
+        return
+    S = T.sem
+
+    def peers(c):
+        return [d for d in T.cores if d != c and topo.chip(d) == topo.chip(c)]
+
+    def step1_dsts(c):
+        return peers(c) + ([HELPER_FEED[c]] if c in HELPER_FEED else [])
+
+    def multicast(dsts, lo, hi, sem):
+        g.remote_dma_fused([RemoteDMATransfer(
+            dst_ids=[DstId(rid=topo.addr(d)[0], pnc=topo.addr(d)[1]) for d in dsts],
+            dma_engine_mask=0xFFFF, remote_sem=sem,
+            srcs=[T.g[:, lo:hi]], dsts=[T.g[:, lo:hi] for d in dsts])], local_sem=S.sent)
+
+    sent = 0
+    if rank is not None:
+        g.dma_start(T.g[:, B * rank:B * rank + B], T.x[:, :]).then_inc(S.ld, 16)
+        g.wait_ge(S.ld, 16)
+        multicast(step1_dsts(core), B * rank, B * rank + B, S.on)
+        sent += 16
+
+    n_on = 16 * sum(1 for c in T.cores if core in step1_dsts(c))
+    g.wait_ge(S.on, n_on)
+
+    if core in CROSS:
+        b0, dst = CROSS[core]
+        rid, pid, _se = topo.addr(dst)
+        g.remote_dma(T.g[:, B * b0:B * b0 + 2 * B], T.g[:, B * b0:B * b0 + 2 * B], S.xc, S.sent, pid, rid,
+                     topo.mask(core, dst))
+        sent += 8
+
+    landed = [b0 for (b0, dst) in CROSS.values() if dst == core]
+    if landed:
+        g.wait_ge(S.xc, 8)
+        multicast(peers(core), B * landed[0], B * landed[0] + 2 * B, S.fan)
+        sent += 16
+
+    if rank is not None:
+        n_fan = 16 * sum(1 for (b0, dst) in CROSS.values() if dst != core and topo.chip(dst) == topo.chip(core))
+        g.wait_ge(S.fan, n_fan)
+        g.dma_start(T.y[:, :], T.g[:, :]).then_inc(S.st, 16)
+        g.wait_ge(S.st, 16)
+    g.wait_ge(S.sent, sent)

@@ -3,57 +3,70 @@ from concourse.bass import DstId, RemoteDMATransfer
 SCRATCH = {
     "g": ("sbuf", [128, 96], "bfloat16"),
 }
-SEMAPHORES = ["ld", "st", "on", "xc", "fan", "sent"]
+SEMAPHORES = ["ld", "st", "r1", "r2", "r3", "sent"]
 
 B = 8
-CROSS = {74: (0, 64), 75: (2, 65), 78: (4, 66), 79: (6, 67), 67: (10, 72), 70: (8, 76)}
-HELPER_FEED = {64: 70, 65: 70}
+ALL = 0xFFFF
+Q0, Q1, Q2, Q3 = 0x000F, 0x00F0, 0x0F00, 0xF000
+
+PLAN = {
+    1: {
+        72: [[(0, 1, [74, 73], ALL)]], 73: [[(1, 2, [74], ALL)]], 75: [[(3, 4, [74], ALL)]],
+        76: [[(4, 5, [78, 77], ALL)]], 77: [[(5, 6, [78], ALL)]], 79: [[(7, 8, [78], ALL)]],
+        64: [[(8, 9, [70, 67, 65], ALL)]], 65: [[(9, 10, [70, 67], ALL)]],
+        66: [[(10, 11, [70, 67], ALL)]], 67: [[(11, 12, [70, 66], ALL)]],
+    },
+    2: {
+        74: [[(0, 4, [68], Q0)], [(1, 4, [72], Q1), (0, 3, [75], Q2)], [(2, 4, [73], Q3)]],
+        78: [[(4, 8, [69], Q0)], [(5, 8, [76], Q1), (4, 7, [79], Q2)], [(6, 8, [77], Q3)]],
+        70: [[(8, 12, [79], Q0)], [(9, 12, [64], Q1)], [(10, 12, [65], Q2), (8, 10, [66], Q3)]],
+        67: [[(8, 12, [75], 0x00FF)]],
+    },
+    3: {
+        72: [[(0, 4, [76, 77], ALL)]], 73: [[(0, 4, [78, 79], ALL)]], 75: [[(8, 12, [72, 73, 74], ALL)]],
+        76: [[(4, 8, [72, 73], ALL)]], 77: [[(4, 8, [74, 75], ALL)]], 79: [[(8, 12, [76, 77, 78], ALL)]],
+        68: [[(0, 4, [64, 65, 66, 67], ALL)]], 69: [[(4, 8, [64, 65, 66, 67], ALL)]],
+    },
+}
+
+
+def engines(mask):
+    return bin(mask).count("1")
+
+
+def lands(core, rnd):
+    return sum(engines(m) for calls in PLAN[rnd].values() for call in calls
+               for (lo, hi, dsts, m) in call if core in dsts)
 
 
 def rank_program(g, core, T, topo):
     rank = T.rank_of(core)
-    if rank is None and core != 70:
+    if rank is None and not any(core in PLAN[r] for r in PLAN):
         return
     S = T.sem
+    rsem = {1: S.r1, 2: S.r2, 3: S.r3}
 
-    def peers(c):
-        return [d for d in T.cores if d != c and topo.chip(d) == topo.chip(c)]
-
-    def step1_dsts(c):
-        return peers(c) + ([HELPER_FEED[c]] if c in HELPER_FEED else [])
-
-    def multicast(dsts, lo, hi, sem):
-        g.remote_dma_fused([RemoteDMATransfer(
-            dst_ids=[DstId(rid=topo.addr(d)[0], pnc=topo.addr(d)[1]) for d in dsts],
-            dma_engine_mask=0xFFFF, remote_sem=sem,
-            srcs=[T.g[:, lo:hi]], dsts=[T.g[:, lo:hi] for d in dsts])], local_sem=S.sent)
+    if rank is not None:
+        g.sync.dma_start(T.g[:, B * rank:B * rank + B], T.x[:, :]).then_inc(S.ld, 16)
+        g.wait_ge(S.ld, 16)
 
     sent = 0
-    if rank is not None:
-        g.dma_start(T.g[:, B * rank:B * rank + B], T.x[:, :]).then_inc(S.ld, 16)
-        g.wait_ge(S.ld, 16)
-        multicast(step1_dsts(core), B * rank, B * rank + B, S.on)
-        sent += 16
-
-    n_on = 16 * sum(1 for c in T.cores if core in step1_dsts(c))
-    g.wait_ge(S.on, n_on)
-
-    if core in CROSS:
-        b0, dst = CROSS[core]
-        rid, pid, _se = topo.addr(dst)
-        g.remote_dma(T.g[:, B * b0:B * b0 + 2 * B], T.g[:, B * b0:B * b0 + 2 * B], S.xc, S.sent, pid, rid,
-                     topo.mask(core, dst))
-        sent += 8
-
-    landed = [b0 for (b0, dst) in CROSS.values() if dst == core]
-    if landed:
-        g.wait_ge(S.xc, 8)
-        multicast(peers(core), B * landed[0], B * landed[0] + 2 * B, S.fan)
-        sent += 16
-
-    if rank is not None:
-        n_fan = 16 * sum(1 for (b0, dst) in CROSS.values() if dst != core and topo.chip(dst) == topo.chip(core))
-        g.wait_ge(S.fan, n_fan)
-        g.dma_start(T.y[:, :], T.g[:, :]).then_inc(S.st, 16)
-        g.wait_ge(S.st, 16)
+    for rnd in (1, 2, 3):
+        for call in PLAN[rnd].get(core, []):
+            g.remote_dma_fused([RemoteDMATransfer(
+                dst_ids=[DstId(rid=topo.addr(d)[0], pnc=topo.addr(d)[1]) for d in dsts],
+                dma_engine_mask=m, remote_sem=rsem[rnd],
+                srcs=[T.g[:, B * lo:B * hi]], dsts=[T.g[:, B * lo:B * hi] for d in dsts])
+                for (lo, hi, dsts, m) in call], local_sem=S.sent)
+            sent += sum(engines(m) for (lo, hi, dsts, m) in call)
+        if lands(core, rnd):
+            g.wait_ge(rsem[rnd], lands(core, rnd))
     g.wait_ge(S.sent, sent)
+
+    if rank is not None:
+        g.sync.wait_ge(S.ld, 16)
+        for rnd in (1, 2, 3):
+            if lands(core, rnd):
+                g.sync.wait_ge(rsem[rnd], lands(core, rnd))
+        g.sync.dma_start(T.y[:, :], T.g[:, :]).then_inc(S.st, 16)
+        g.sync.wait_ge(S.st, 16)

from concourse.bass import DstId, RemoteDMATransfer

SCRATCH = {
    "g": ("sbuf", [128, 96], "bfloat16"),
}
SEMAPHORES = ["ld", "st", "r1", "r2", "r3", "sent"]

B = 8
ALL = 0xFFFF
Q0, Q1, Q2, Q3 = 0x000F, 0x00F0, 0x0F00, 0xF000

PLAN = {
    1: {
        72: [[(0, 1, [74, 73], ALL)]], 73: [[(1, 2, [74], ALL)]], 75: [[(3, 4, [74], ALL)]],
        76: [[(4, 5, [78, 77], ALL)]], 77: [[(5, 6, [78], ALL)]], 79: [[(7, 8, [78], ALL)]],
        64: [[(8, 9, [70, 67, 65], ALL)]], 65: [[(9, 10, [70, 67], ALL)]],
        66: [[(10, 11, [70, 67], ALL)]], 67: [[(11, 12, [70, 66], ALL)]],
    },
    2: {
        74: [[(0, 4, [68], Q0)], [(1, 4, [72], Q1), (0, 3, [75], Q2)], [(2, 4, [73], Q3)]],
        78: [[(4, 8, [69], Q0)], [(5, 8, [76], Q1), (4, 7, [79], Q2)], [(6, 8, [77], Q3)]],
        70: [[(8, 12, [79], Q0)], [(9, 12, [64], Q1)], [(10, 12, [65], Q2), (8, 10, [66], Q3)]],
        67: [[(8, 12, [75], 0x00FF)]],
    },
    3: {
        72: [[(0, 4, [76, 77], ALL)]], 73: [[(0, 4, [78, 79], ALL)]], 75: [[(8, 12, [72, 73, 74], ALL)]],
        76: [[(4, 8, [72, 73], ALL)]], 77: [[(4, 8, [74, 75], ALL)]], 79: [[(8, 12, [76, 77, 78], ALL)]],
        68: [[(0, 4, [64, 65, 66, 67], ALL)]], 69: [[(4, 8, [64, 65, 66, 67], ALL)]],
    },
}


def engines(mask):
    return bin(mask).count("1")


def lands(core, rnd):
    return sum(engines(m) for calls in PLAN[rnd].values() for call in calls
               for (lo, hi, dsts, m) in call if core in dsts)


def rank_program(g, core, T, topo):
    rank = T.rank_of(core)
    if rank is None and not any(core in PLAN[r] for r in PLAN):
        return
    S = T.sem
    rsem = {1: S.r1, 2: S.r2, 3: S.r3}

    if rank is not None:
        g.sync.dma_start(T.g[:, B * rank:B * rank + B], T.x[:, :]).then_inc(S.ld, 16)
        g.wait_ge(S.ld, 16)

    sent = 0
    for rnd in (1, 2, 3):
        for call in PLAN[rnd].get(core, []):
            g.remote_dma_fused([RemoteDMATransfer(
                dst_ids=[DstId(rid=topo.addr(d)[0], pnc=topo.addr(d)[1]) for d in dsts],
                dma_engine_mask=m, remote_sem=rsem[rnd],
                srcs=[T.g[:, B * lo:B * hi]], dsts=[T.g[:, B * lo:B * hi] for d in dsts])
                for (lo, hi, dsts, m) in call], local_sem=S.sent)
            sent += sum(engines(m) for (lo, hi, dsts, m) in call)
        if lands(core, rnd):
            g.wait_ge(rsem[rnd], lands(core, rnd))
    g.wait_ge(S.sent, sent)

    if rank is not None:
        g.sync.wait_ge(S.ld, 16)
        for rnd in (1, 2, 3):
            if lands(core, rnd):
                g.sync.wait_ge(rsem[rnd], lands(core, rnd))
        g.sync.dma_start(T.y[:, :], T.g[:, :]).then_inc(S.st, 16)
        g.sync.wait_ge(S.st, 16)
